import numpy as np, ml_dtypes
CORES = [66,74,82,90,194,202,210,218]
N = 8
BF = ml_dtypes.bfloat16
def gentries(a):
    return np.ascontiguousarray(a.reshape(8, 16, -1).transpose(0, 2, 1)).reshape(8, -1)
def gtable(e):
    e = np.asarray(e); return np.ascontiguousarray(e.reshape(8, -1, 16).transpose(0, 2, 1)).reshape(128, -1).astype(np.int32)
IT, M, CAP, ST, RO = 2048, 1024, 128, 4, 3
def forest(rng):
    k = np.full((N, 8, 2, M), M, np.int64); par = np.zeros((N, 8, M), np.int64); m = M // 8
    for q in range(N):
        for g in range(8):
            p = rng.permutation(M).reshape(8, m); par[q, g, p[1::2].reshape(-1)] = 1
            for l in range(7):
                u = rng.permutation(2 * m)[:m]; k[q, g, u // m, p[l, u % m]] = p[l + 1]
    return k, par
def labels(rng, e):
    lab = np.full((N, 8, IT), M, np.int64)
    for q in range(N):
        for g in range(8):
            n = int(e[q, g]); live = rng.permutation(M)[:n]; o = rng.permutation(IT)
            w = live[np.minimum((n * rng.random(IT - n) ** 2).astype(np.int64), n - 1)]
            lab[q, g, o[:n]] = live; lab[q, g, o[n:]] = np.where(rng.random(IT - n) < 0.06, M, w)
    return lab
def lot(rng, live):
    o = rng.permutation(IT); n = len(live); lab = np.full(IT, M, np.int64)
    lab[o[:n]] = live; lab[o[n:]] = np.where(rng.random(IT - n) < 0.06, M, live[rng.integers(0, n, IT - n)])
    return lab
def count(rng):
    return rng.integers(M * 5 // 8, M * 7 // 8, (N, 8))
def parts(rng, lab=None):
    if lab is None: lab = labels(rng, count(rng))
    k, par = forest(rng); n = np.zeros((N, 8, IT), np.int64); cur = np.zeros((N, 8, M), np.int64); siz = np.zeros((N, 8, M), np.int64)
    for q in range(N):
        for g in range(8):
            o = rng.permutation(IT); o = o[np.argsort(lab[q, g, o], kind="stable")]; s = lab[q, g, o]
            last = np.append(s[1:] != s[:-1], True)
            n[q, g, o] = np.where(last, o[np.searchsorted(s, s)], np.roll(o, -1))
            z = np.bincount(s, minlength=M + 1)[:M]; a = np.minimum(np.searchsorted(s, np.arange(M)), IT - 1)
            siz[q, g] = z; cur[q, g] = np.where(z > 0, o[a], rng.integers(0, IT, M))
    tgt = np.minimum(np.maximum(siz + rng.integers(-2, 4, siz.shape), 0), IT)
    return {"k": k, "par": par, "n": n, "cur": cur, "siz": siz, "tgt": tgt}
def values(rng):
    h = rng.choice(np.array([60, 90, 140, 230]), (N, 8, 1, 1))
    x = np.clip(rng.integers(40, 215, (N, 8, 1, IT)) + rng.integers(-40, 41, (N, 8, 16, IT)), 0, 254)
    key = np.clip((h * rng.random((N, 8, 1, M))).astype(np.int64) + rng.integers(-40, 41, (N, 8, 16, M)), 0, 254)
    return x, key
def pack(d, x, key):
    tab = lambda a: np.stack([gtable(b) for b in a])
    key = np.where(d["siz"][:, :, None, :] > 0, key, 255)
    return {"x": np.ascontiguousarray(x.reshape(N, 128, IT)).astype(np.float32).astype(BF), "ky": np.ascontiguousarray(key.reshape(N, 128, M)).astype(np.float32).astype(BF),
            "nxt": d["n"].astype(np.int32), "cur": tab(d["cur"]), "siz": tab(d["siz"]), "tgt": tab(d["tgt"]), "par": tab(d["par"]), "kl": tab(d["k"][:, :, 0]), "kr": tab(d["k"][:, :, 1])}
def setup_inputs(rng):
    d = parts(rng); x, key = values(rng)
    return pack(d, x, key)
def setup_inputs_room(rng):
    d = parts(rng); d["tgt"] = np.where(d["par"] == 0, 0, d["tgt"])
    x = rng.integers(40, 201, (N, 8, 16, IT)); key = rng.integers(0, 40, (N, 8, 16, M))
    for q in range(N):
        for g in range(8):
            live = rng.permutation(np.nonzero(d["siz"][q, g])[0]); e = len(live)
            n = int(rng.choice(np.array([0, 1, CAP - 1, CAP, CAP + 1, e])))
            if q == 0: n = (CAP, CAP + 1, e, CAP - 1, 1, 0, CAP, CAP + 1)[g]
            if q == 1: n = (CAP + 1, CAP, CAP, e, CAP, CAP, 0, 1)[g]
            key[q, g][:, live[:n]] = rng.integers(201, 255, (16, n))
    return pack(d, x, key)
def setup_inputs_ties(rng):
    d = parts(rng); c = np.array([0, 7, 8, 9, 16])
    place = np.argsort(rng.random((N, 8, 16, 1)), axis=2)
    a = rng.choice(c, (N, 8, 1, IT)); w = rng.integers(1, 100, (N, 8, 16, IT)) * (rng.random((N, 8, 1, IT)) < 0.8)
    x = np.where(place < a, 100 - w, 100 + w)
    key = 100 + (place < rng.choice(c, (N, 8, 1, M))).astype(np.int64); key[:, ::2] = 100
    return pack(d, x, key)
def setup_inputs_ends(rng):
    e = count(rng); e[:, 2] = M; e[:, 3] = M // 16; lab = labels(rng, e)
    for q in range(N):
        n = int(e[q, 0]); lab[q, 0] = M; lab[q, 0, rng.permutation(IT)[:n]] = rng.permutation(M)[:n]
        live = rng.permutation(M)[:M // 4]; lab[q, 1] = live[0]; lab[q, 1, rng.permutation(IT)[:M // 4]] = live
    d = parts(rng, lab); d["k"][:, 4, 0] = M; d["k"][:, 5, 1] = M; h = M // 2
    for q in range(N):
        a = rng.permutation(M); d["k"][q, 7] = M; d["k"][q, 7, 0, a[:h]] = a[h:]; d["k"][q, 7, 1, a[h:]] = a[:h]
        d["par"][q, 7, a[:h]] = 0; d["par"][q, 7, a[h:]] = 1
        for g, b in ((4, 0), (5, 1)):
            k = d["k"][q, g]; lone = np.all(k == M, axis=0); lone[k[k < M]] = False; d["par"][q, g, lone] = b
    z = d["siz"]; u = rng.integers(0, 4, z.shape); big = np.argmax(z[:, 1], axis=1); r = np.arange(N)
    for q in range(N):
        w = np.nonzero((z[q, 1] > 0) & (d["par"][q, 1] != d["par"][q, 1, big[q]]))[0]
        if len(w) > 0:
            w = int(rng.choice(w)); k = d["k"][q, 1]; k[(k == big[q]) | (k == w)] = M
            k[0, big[q]] = w; k[1, big[q]] = M
    d["tgt"] = np.where(u == 0, 0, np.where(u == 1, z, np.where(u == 2, np.minimum(z + 1, IT), IT)))
    d["tgt"][r, 1, big] = z[r, 1, big] + 1 - r % 2
    x, key = values(rng)
    return pack(d, x, key)
def setup_inputs_full(rng):
    h = M // 2; m = M // 4; lab = labels(rng, count(rng)); a = np.argsort(rng.random((N, 8, M)), axis=2); top = np.zeros((N, 5), np.int64)
    for q in range(N):
        for g, w in ((0, a[q, 0]), (1, a[q, 1, h:]), (2, a[q, 2]), (3, a[q, 3]), (4, np.concatenate([a[q, 4, :m // 2], a[q, 4, m:2 * m], a[q, 4, 3 * m:]]))):
            lab[q, g] = lot(rng, w)
        lab[q, 5] = a[q, 5, 1]; lab[q, 5, rng.permutation(IT)[:(IT - 1, IT, IT - 1, IT - 2)[q % 4]]] = a[q, 5, 0]
        lab[q, 6] = a[q, 6, 15:][rng.integers(0, M - 15, IT)]; o = rng.permutation(IT); at = 0
        for f in range(5):
            kid = int(rng.integers(1, 41)); s = IT // 8 + 45 + 4 * int(rng.integers(0, 14)) + 2 * (f % 2); top[q, f] = s + f % 2
            for v, n in ((f, s - kid), (5 + f, kid), (10 + f, kid)):
                lab[q, 6, o[at:at + n]] = a[q, 6, v]; at += n
    d = parts(rng, lab); k, par, t, z = d["k"], d["par"], d["tgt"], d["siz"]; k[:, :7] = M
    x, key = values(rng)
    for g in (0, 1, 2, 4): t[:, g] = np.minimum(z[:, g] + rng.integers(1, 50, (N, M)), IT)
    x[:, 3] = rng.integers(40, 201, (N, 16, IT)); key[:, 3] = rng.integers(0, 40, (N, 16, M))
    x[:, 4] = np.where(rng.random((N, 1, IT)) < 0.3, 254, rng.integers(200, 255, (N, 16, IT)))
    for q in range(N):
        for g in (0, 1):
            b = (q + g) % 2; k[q, g, rng.integers(0, 2, h), a[q, g, :h]] = a[q, g, h:]
            par[q, g, a[q, g, :h]] = b; par[q, g, a[q, g, h:]] = 1 - b
        w = rng.permutation(M - 16)[:16]; k[q, 2, rng.integers(0, 2, 16), np.arange(M - 16, M)] = w
        par[q, 2] = q % 2; par[q, 2, w] = 1 - q % 2
        key[q, 3][:, int(rng.integers(0, 16))::16] = rng.integers(201, 255, (16, M // 16))
        p = a[q, 4]; b = (q // 2) % 2; k[q, 4, 1, p[:m]] = p[m:2 * m]; k[q, 4, 0, p[:m:2]] = p[2 * m:3 * m:2]
        par[q, 4, p[:m]] = b; par[q, 4, p[m:3 * m]] = 1 - b
        c = np.where(rng.random(m) < 0.5, 16, rng.integers(9, 17, m)); place = np.argsort(rng.random((16, m)), axis=0)
        key[q, 4][:, p[m:2 * m]] = np.where(place < c, 254, rng.integers(100, 255, (16, m)))
        key[q, 4][:, p[3 * m:3 * m + m // 2]] = 254
        b = int(rng.integers(0, 2)); u, w = int(a[q, 5, 0]), int(a[q, 5, 1]); k[q, 5, int(rng.integers(0, 2)), u] = w
        par[q, 5, u] = b; par[q, 5, w] = 1 - b; t[q, 5, u] = (IT, IT, IT - 1, IT - 1)[q % 4]
        p = a[q, 6]; k[q, 6, 0, p[:5]] = p[5:10]; k[q, 6, 1, p[:5]] = p[10:15]
        par[q, 6, p[:5]] = 0; par[q, 6, p[5:15]] = 1; t[q, 6, p[:5]] = top[q]
    return pack(d, x, key)
def setup_inputs_spread(rng):
    d = parts(rng)
    d["tgt"] = np.minimum(np.exp2(13 * rng.random((N, 8, M))).astype(np.int64) - 1, IT)
    x = np.minimum((np.exp2(8 * rng.random((N, 8, 1, IT))) * rng.random((N, 8, 16, IT))).astype(np.int64), 254)
    key = np.minimum((np.exp2(8 * rng.random((N, 8, 1, M))) * rng.random((N, 8, 16, M))).astype(np.int64), 254)
    return pack(d, x, key)
def check_inputs(d):
    bad = []
    for k, hi in (("x", 254), ("ky", 255)):
        a = np.asarray(d[k]).astype(np.float32)
        if not np.all((a >= 0) & (a <= hi) & (a == np.floor(a))): bad.append("whole numbers and range of " + k)
    for k, hi in (("nxt", IT - 1), ("cur", IT - 1), ("siz", IT), ("tgt", IT), ("par", 1), ("kl", M), ("kr", M)):
        if np.min(d[k]) < 0 or np.max(d[k]) > hi: bad.append("range of " + k)
    if bad: return bad
    n = np.asarray(d["nxt"]).astype(np.int64)
    if np.any(np.sort(n, axis=2) != np.arange(IT)): return ["every item once in a row of nxt"]
    cur, siz, par, kl, kr = [np.stack([gentries(a) for a in d[k]]).astype(np.int64) for k in ("cur", "siz", "par", "kl", "kr")]
    live = siz > 0; key = np.asarray(d["ky"]).astype(np.float32).reshape(N, 8, 16, M)
    if np.any(np.where(live[:, :, None, :], key > 254, key != 255)): bad.append("keys of empty and of other nodes")
    lab = np.tile(np.arange(IT), (N, 8, 1)); j = n
    for i in range((IT - 1).bit_length()):
        lab = np.minimum(lab, np.take_along_axis(lab, j, 2)); j = np.take_along_axis(j, j, 2)
    def tally(a, w, k):
        a = (a + np.arange(N * 8).reshape(N, 8, 1) * k)[w]
        return np.bincount(a, minlength=N * 8 * k).reshape(N, 8, k)
    c = tally(lab, np.ones(lab.shape, bool), IT); own = np.take_along_axis(lab, cur, 2)
    if np.any(live & (np.take_along_axis(c, own, 2) != siz)): bad.append("sizes are the rings' numbers of items")
    if np.max(tally(own, live, IT)) > 1: bad.append("nodes that aren't empty have different rings")
    kids = np.concatenate([kl, kr], axis=2)
    if np.max(tally(kids, kids < M, M)) > 1: bad.append("a node stands at most once in kl and kr")
    px = np.concatenate([par, np.full((N, 8, 1), 2, np.int64)], axis=2)
    if np.any(np.take_along_axis(px, kids, 2) == np.concatenate([par, par], axis=2)): bad.append("parities of kids")
    return bad
def reference(x, ky, nxt, cur, siz, tgt, par, kl, kr):
    X = x.astype(np.float32).reshape(N, 8, 16, IT)
    K = np.concatenate([ky.astype(np.float32).reshape(N, 8, 16, M), np.full((N, 8, 16, 1), 255, np.float32)], axis=3)
    nx = nxt.astype(np.int64)
    C, Z, T, P, A, B = [np.stack([gentries(a) for a in b]).astype(np.int64) for b in (cur, siz, tgt, par, kl, kr)]
    none = np.zeros((N, 8, 1), np.int64); C = np.concatenate([C, none], axis=2); Z = np.concatenate([Z, none], axis=2)
    for t in range(RO):
        le = np.take_along_axis(K, A[:, :, None, :], 3) <= np.take_along_axis(K, B[:, :, None, :], 3)
        ch = np.where(np.add.reduce(le, axis=2, dtype=np.int64) >= 9, A, B)
        go = (P == t % 2) & (Z[..., :M] < T) & (np.take_along_axis(Z, ch, 2) > 0)
        i, j, v = np.nonzero(go & (Z[..., :M] > 0)); c = ch[i, j, v]
        a, b = C[i, j, v], C[i, j, c]; na, nb = nx[i, j, a], nx[i, j, b]
        nx[i, j, a] = nb; nx[i, j, b] = na
        i, j, v = np.nonzero(go); c = ch[i, j, v]
        C[i, j, v] = np.where(Z[i, j, v] > 0, C[i, j, v], C[i, j, c])
        K[i, j, :, v] = K[i, j, :, c]; K[i, j, :, c] = 255
        Z[i, j, v] = Z[i, j, v] + Z[i, j, c]; Z[i, j, c] = 0
        live = Z[..., :M] > 0; s = C[..., :M]; lv = np.full((N, 8, M), -1, np.int64)
        for k in range(ST):
            s = np.take_along_axis(nx, s, 2)
            low = np.take_along_axis(X, s[:, :, None, :], 3) < K[..., :M]
            lv = np.where((lv < 0) & live & (np.add.reduce(low, axis=2, dtype=np.int64) >= 9), s, lv)
        C[..., :M] = np.where(live, s, C[..., :M])
        has = (lv >= 0).astype(np.int64); pl = np.add.accumulate(has, axis=2) - 1
        i, j, v = np.nonzero((has == 1) & (pl < CAP))
        e = np.full((N, 8, CAP), -1, np.int64); e[i, j, pl[i, j, v]] = lv[i, j, v]
        come = np.roll(np.take_along_axis(X, np.maximum(e, 0)[:, :, None, :], 3), 1, axis=0)
        i, j, k = np.nonzero((e >= 0) & (np.roll(e, 1, axis=0) >= 0))
        X[i, j, :, e[i, j, k]] = come[i, j, :, k]
    return {"yx": X.reshape(N, 128, IT).astype(BF), "yk": np.ascontiguousarray(K[..., :M]).reshape(N, 128, M).astype(BF), "yn": nx.astype(np.float32),
            "yc": np.stack([gtable(a) for a in np.ascontiguousarray(C[..., :M])]).astype(np.float32)}

from concourse.mybir import AluOpType as A, ActivationFunctionType as F

IT, M, RO = 2048, 1024, 3
BIG = 65536.0
BASE = 8 * BIG
HUGE = 2097152.0
OFF = 32.0 * 129
CFG = {"sch": 2, "off": ((2, 1, 0), (2, 1, 1)), "acc": (0, 0, 4), "patch": (), "wch": (0, 2)}
ORDER = [6,7,13,65,1,4,0,3,2,5,47,53,46,51,62,54,63,60,56,57,36,59,64,9,83,10,82,14,18,70,19,87,88,8,89,99,20,84,73,21,22,90,100,91,101,11,15,48,12,23,50,24,66,102,26,29,103,25,31,33,85,32,104,105,41,27,86,44,61,74,71,107,106,110,109,108,115,111,92,76,116,42,112,30,49,117,43,113,118,67,75,72,218,114,219,28,52,126,55,34,93,129,58,220,35,45,130,94,95,16,98,119,68,222,69,131,132,39,133,134,137,145,135,79,77,136,221,17,138,142,139,140,96,223,80,224,97,120,121,37,122,38,226,81,78,225,143,228,227,229,123,141,230,234,146,231,40,232,124,147,233,144,125,173,238,150,239,174,149,153,127,128,235,148,151,154,242,157,246,241,236,240,152,177,156,160,155,161,247,176,158,164,175,180,237,167,243,248,244,168,159,183,254,178,163,249,179,319,165,245,181,166,318,321,217,320,322,323,182,324,251,162,169,184,326,329,328,325,327,334,330,185,170,186,394,189,331,187,188,171,255,190,172,191,252,198,193,197,194,199,196,202,192,195,200,201,203,204,253,332,205,206,207,256,333,208,258,213,259,209,210,211,257,335,260,212,262,214,215,336,216,339,277,261,263,344,338,337,345,264,274,266,276,346,265,340,267,347,273,341,352,268,275,283,278,269,317,348,279,280,270,342,282,281,349,250,284,271,272,343,285,350,286,289,287,290,288,353,291,302,293,292,295,297,298,296,294,299,300,351,301,303,304,305,354,355,306,307,356,379,378,309,308,310,311,312,357,358,359,313,360,363,361,362,364,365,314,315,366,380,316,367,370,397,388,372,396,391,389,368,400,371,392,399,390,374,393,373,375,403,382,395,381,398,402,401,369,376,383,377,404,385,384,386,405,387,406,409,407,410,408,411,423,418,415,420,413,419,412,421,414,416,417,422,424,425,426,427,428,430,429,434,431,432,433,435,436,437,438]

BF, FP = "bfloat16", "float32"
SCRATCH = {"LF": ("sbuf", [128, 64 * 70], FP), "LB": ("sbuf", [128, 64 * 40], BF), "LH": ("sbuf", [128, 64 * 30], "float16"),
           "LU": ("sbuf", [128, 64 * 40], "uint16"), "LI": ("sbuf", [128, 64 * 16], "int32"),
           "NI32": ("sbuf", [128, 128], "int32"), "NT32": ("sbuf", [128, 256], "int32"), "COLI": ("sbuf", [128, 16], "int32"),
           "SEL": ("sbuf", [128, 128], "float16")}
for _w, _d, _names in (
        (2192, BF, "X"), (3088, FP, "NX"), (1024, FP, "NQ"), (1024, BF, "ZW IOA IOB KL LE ZG NP SG0 SG1 XG0 XG1 CM0 CM1 CM2 CM3"),
        (128, FP, "NLO NHI OLO OHI"), (256, BF, "OB NLS"), (256, FP, "OF RS GS"), (64, BF, "ZLO ZHI"), (64, FP, "YC COL"),
        (144, FP, "WQ"), (144, BF, "UI W1 WV WH WN WS"), (512, BF, "KEEP KRAW F8 CNT"), (16, BF, "SENT"), (16, FP, "SENTF"),
        (128, BF, "IP IN IH INH I64 I1k IN1k I2k T2 BO UP KIO EQ SND0 SND1 SND2 RCV0 RCV1 RCV2"), (384, BF, "DD"),
        (320, FP, "M5 SC0 SC1 SC2"), (64, "int32", "i_cur i_siz i_tgt i_par i_kl i_kr"),
        (1040, BF, "K0 K1 K2 K3 NR0 NR1 NR2"), (3072, BF, "PM0 PM1 PM2")):
    for _n in _names.split():
        SCRATCH[_n] = ("sbuf", [128, _w], _d)
for _t in range(8):
    SCRATCH["P%d" % _t] = ("psum", [128, 512], FP)
SEMAPHORES = ["ev", "ea", "ep", "eg", "sent"] + ["arr%d" % t for t in range(RO)] + ["d%d" % i for i in range(30)]


def build(T, send, cfg):
    ops = []
    pools = {"LF": {}, "LB": {}, "LH": {}, "LU": {}, "LI": {}}

    def tile(pool, name, lo=0, hi=64):
        d = pools[pool]
        if name not in d:
            d[name] = 64 * len(d)
        return T[pool][:, d[name] + lo:d[name] + hi]

    def op(eng, fn, r, w, c):
        ops.append({"eng": eng, "fn": fn, "r": list(r), "w": list(w), "c": c})

    def f(n, lo=0, hi=64): return (tile("LF", n, lo, hi), ["f" + n])
    def b(n, lo=0, hi=64): return (tile("LB", n, lo, hi), ["b" + n])
    def h(n, lo=0, hi=64): return (tile("LH", n, lo, hi), ["h" + n])
    def u(n): return (tile("LU", n), ["u" + n + "#0", "u" + n + "#1"])
    def u8(n): return (tile("LU", n, 0, 8), ["u" + n])
    def i32(n): return (tile("LI", n), ["i" + n])
    def buf(n, lo=None, hi=None, step=1, key=None): return (T[n][:, lo:hi:step], key or [n])
    def col(j): return (T.COL[:, j:j + 1], ["col%d" % j])
    def ps(bank, lo=0, hi=64): return (T[bank][:, lo:hi], [bank])
    def two(n): return [n + "#0", n + "#1"]

    def split(vals):
        r, v = [], []
        for s in vals:
            if isinstance(s, tuple):
                r += s[1]
                v.append(s[0])
            else:
                v.append(s)
        return r, v

    def ts(out, a, s1, s2, o0, o1=None, n=64):
        r, v = split((s1, s2))
        if o1 is None:
            op("v", lambda q: q.tensor_scalar(out[0], a[0], v[0], None, o0), a[1] + r, out[1], ("e", n))
        else:
            op("v", lambda q: q.tensor_scalar(out[0], a[0], v[0], v[1], o0, o1), a[1] + r, out[1], ("e", n))

    def tt(out, a, c, o, n=128, kind="e"):
        op("v", lambda q: q.tensor_tensor(out[0], a[0], c[0], o), a[1] + c[1], out[1], (kind, n))

    def cp(out, a, n=64, kind="e"):
        op("v", lambda q: q.tensor_copy(out[0], a[0]), a[1], out[1], (kind, n))

    def ms(out, val, n=64):
        op("v", lambda q: q.memset(out[0], val), [], out[1], ("e", n))

    def act(out, a, scale=1.0, bias=0.0, n=64, fn=F.Identity):
        r, v = split((scale, bias))
        op("a", lambda q: q.activation(out[0], a[0], fn, bias=v[1], scale=v[0]), a[1] + r, out[1], ("e", n))

    def plain(out, a, fn, c):
        op("a", lambda q: q.activation(out[0], a[0], fn), a[1], out[1], c)

    def scan(out, d0, d1, o0, o1, n):
        op("v", lambda q: q.tensor_tensor_scan(out[0], d0[0], d1[0], 0.0, o0, o1), d0[1] + d1[1], out[1], ("e", n))

    def iota(out, pat, base, ch, n, flt=True):
        if flt:
            op("g", lambda q: q.iota(out[0], pat, base, ch, allow_small_or_imprecise_dtypes=True), [], out[1], ("i", n))
        else:
            op("g", lambda q: q.iota(out[0], pat, base, ch), [], out[1], ("i", n))

    def dma(eng, o, a, r, w, nbytes):
        op(eng, lambda q: q.dma_start(o, a), r, w, ("d", nbytes))

    def pieces(name, lst, win, n):
        out = []
        for j in range(n):
            w = 64 // n
            ks = (0, 1) if n == 1 else (j * 2 // n,)
            out.append(((T[name][:, 16 * w * j:16 * w * (j + 1)], ["%s#%d" % (name, i) for i in ks]),
                        (win[0].indirect(tile("LU", lst, w * j, w * (j + 1))), win[1], ["u%s#%d" % (lst, i) for i in ks]), 16 * w))
        return out

    def gather_a(dst, win, lst, n=1):
        for o, (src, wk, lk), c in pieces(dst, lst, win, n):
            plain(o, (src, wk + lk), F.Copy, ("g", c))

    def scatter(eng, win, lst, src, n):
        for a, (o, wk, lk), c in pieces(src, lst, win, n):
            if eng == "v":
                cp((o, wk), (a[0], a[1] + lk), c, "s")
            else:
                plain((o, wk), (a[0], a[1] + lk), F.Silu, ("s", c))

    def diag(out, W, src, lo, keys, start, stop, n=64, slow=1):
        def fn(q):
            for i in range(16):
                ins = q.matmul(out[0], T[W][:, 16 - i:144 - i], T[src][:, lo + i:lo + 16 * n:16], start and i == 0, stop and i == 15)
            return ins
        op("p", fn, [W] + keys, out[1], ("p", 1024 * slow))

    def mm(out, terms, start=True, stop=True, n=64):
        def fn(q):
            for j, (W, rhs) in enumerate(terms):
                ins = q.matmul(out[0], T[W][:], rhs[0], start and j == 0, stop and j == len(terms) - 1)
            return ins
        op("p", fn, [k for W, rhs in terms for k in [W] + rhs[1]], out[1], ("p", n * len(terms)))

    for n, e in (("kl", "s"), ("kr", "s"), ("siz", "a"), ("par", "a"), ("tgt", "a"), ("cur", "a")):
        dma(e, T["i_" + n][:], T[n][:], [], ["i_" + n], 32768)
    dma("s", T.K0[:, 0:M], T.ky[:], [], two("K0"), 262144)
    dma("a", T.NI32[:], T.nxt[:], [], ["NI32"], 65536)
    dma("s", T.X[:, 0:IT], T.x[:], two("K0"), ["X"], 524288)
    I = {n: buf("i_" + n) for n in ("cur", "siz", "tgt", "par", "kl", "kr")}

    iota((T.COLI[:, 0:1], ["pi"]), [[0, 1]], 0, 1, 1, False)
    iota(col(1), [[0, 1]], 0, 1, 1)
    iota(buf("UI"), [[1, 144]], -16, 0, 144)
    iota(f("vraw"), [[16, 64]], 0, 1, 64)
    iota(buf("IOB"), [[1, 8], [0, 128]], 1, 0, 1024)
    iota(buf("IOA", key=two("IOA")), [[0, 8], [1, 128]], 0, 0, 1024)
    dma("s", T.IOA[1::16, :], T.IOB[1::16, :], ["IOB"], two("IOA"), 16384)
    iota(buf("T2"), [[16, 8], [0, 16]], 0, 0, 128)
    iota(buf("KIO"), [[1, 128]], 1, 0, 128)
    ts((T.COLI[:, 4:5], ["gi"]), (T.COLI[:, 0:1], ["pi"]), 128 - 16, None, A.bitwise_and)
    cp(col(0), (T.COLI[:, 4:5], ["gi"]))
    tt(col(2), col(1), col(0), A.subtract, 64)
    ts(col(3), col(2), 1.0, 128.0, A.is_equal, A.mult)
    ts(col(4), col(2), 0.0, col(3), A.is_equal, A.add)
    ts(buf("W1"), buf("UI"), col(0), None, A.is_equal, None, 72)
    ts(buf("IP"), buf("UI", 16, 144), col(1), None, A.is_equal)
    act(buf("WV"), buf("W1"), BIG, n=144)
    act(buf("WH"), buf("W1"), col(4), n=144)
    act(buf("WN"), buf("WH"), -1.0, n=144)
    act(buf("WQ"), buf("WH"), n=144)
    for n, w in (("IH", HUGE), ("I64", 64.0), ("I1k", 1024.0), ("IN1k", -1024.0), ("I2k", 2048.0)):
        act(buf(n), buf("IP"), w, n=128)
    if cfg["patch"]:
        act(buf("INH"), buf("IP"), -HUGE, n=128)
    if cfg["off"]:
        act(buf("WS"), buf("W1"), -BIG / 2, n=144)
        act(buf("IN"), buf("IP"), -1.0, n=128)
        ms(b("quart"), BASE / HUGE)
    ts(buf("BO"), buf("T2"), col(0), None, A.is_equal)
    op("g", lambda q: q.affine_select(T.UP[:], T.BO[:], [[-1, 128]], A.is_gt, 0.0, 0, 1), ["BO"], ["UP"], ("i", 128))
    if min(cfg["acc"]) < 8:
        iota(buf("KRAW"), [[0, 8], [1, 64]], 0, 0, 512)
        ts(buf("KEEP"), buf("KRAW"), 1.0, None, A.min, None, 256)
    ts(f("v"), f("vraw"), col(0), None, A.subtract)
    act(f("v128"), f("v"), 1.0, 128.0)
    act(f("v16"), f("v"), 1.0, 16.0)
    act(f("mv"), f("v"), -1.0, 1024.0)
    if max(cfg["acc"]):
        act(f("vh", 0, 8), f("v", 0, 8), 1.0, 0.5)
    ms(b("c200"), 200.0)
    ms(b("c255", 0, 16), 255.0)
    act(col(5), col(3), 0.125, 32.0)
    act(buf("SENT"), buf("UI", 0, 16), 0.0, col(5))
    act(buf("SENTF"), buf("UI", 0, 16), 0.0, col(5))
    for t in range(3):
        act(buf("K%d" % t, M, M + 16, key=["K%ds" % t]), b("c255", 0, 16))
        act(buf("NR%d" % t, M, M + 16, key=["NR%ds" % t]), buf("SENT"))
        ms(buf("SC%d" % t, 0, 320, 5, key=["SC%dz" % t]), 0.0)
    act(buf("X", IT, IT + 16, key=["Xs"]), b("c255", 0, 16))
    plain(buf("NX", IT, IT + 16, key=["NXs"]), buf("SENTF"), F.Silu, ("e", 1400))
    for n in ("P4", "P5"):
        ms(buf(n, 0, 320, 5), 0.0)
    ms(buf("NLS", 0, 256, 4, key=["NLz"]), 0.0)
    ms(buf("PM0", 0, 2048), 0.0, 1024)
    iota(buf("NX", 0, IT, key=["NX", "NX1"]), [[0, 2048]], 0, 0, 2048)
    iota(buf("PM1", 0, 2048), [[0, 2048]], 0, 0, 2048)
    dma("s", T.ZW[:], T.PM1[:, 0:1024], ["PM1"], ["ZW", "ZW1"], 262144)
    dma("s", T.PM2[:, 0:2048], T.PM1[:, 0:2048], ["PM1"], ["PM2"], 524288)

    for j, (o_, s_, dst) in enumerate(((A.bitwise_and, 127, "NLO"), (A.arith_shift_right, 7, "NHI"))):
        ts(buf("NT32", 128 * j, 128 * (j + 1), key=["NT%d" % j]), buf("NI32"), s_, None, o_, None, 128)
        ts(buf(dst), buf("NT32", 128 * j, 128 * (j + 1), key=["NT%d" % j]), 32.0, None, A.add, None, 128)
        dma("s", T.NX[j::16, 0:IT], T[dst][:], [dst], ["NX1" if j else "NX"], 65536)
    for j, (o_, s_, dst) in enumerate(((A.bitwise_and, 127, "ZLO"), (A.arith_shift_right, 7, "ZHI"))):
        ts(i32("z%d" % j), I["siz"], s_, None, o_)
        cp(buf(dst), i32("z%d" % j))
        dma("s", T.ZW[j::16, :], T[dst][:], [dst], ["ZW1" if j else "ZW"], 16384)
    NXK = ["NX", "NX1", "NXs"]
    nxg = (T.NX[:, 0:IT + 16], NXK)
    xg = (T.X[:, 0:IT + 16], ["X", "Xs"])

    cp(u("kl"), I["kl"])
    cp(u("kr"), I["kr"])
    cp(h("kr"), I["kr"])
    tt(f("dlr"), I["kl"], I["kr"], A.subtract)
    tt(f("vk"), f("v"), I["kl"], A.subtract)
    tt(f("T1"), I["tgt"], I["par"], A.mult)
    tt(f("T0"), I["tgt"], f("T1"), A.subtract)
    tt(b("nact0"), I["siz"], f("T0"), A.is_ge)
    ts(b("nl0"), I["siz"], 0.0, None, A.is_equal)
    g0 = buf("RS", 0, 256, 4, key=["RS0"])
    ts(g0, I["cur"], -1.0, 2048.0, A.mult, A.add)
    tt(f("c0a"), b("nl0"), g0, A.mult)
    tt(f("c0b"), f("c0a"), I["cur"], A.add)
    cp(u("s4_-1"), f("c0b"))
    tt(f("c0c"), b("nl0"), f("v16"), A.mult)
    tt(f("c0d"), f("c0c"), f("c0b"), A.add)
    cp(u("sl0"), f("c0d"))

    nl = b("nl0")
    for t in range(RO):
        s = str(t)
        Kt, Kn, PM, NR, SC = "K%d" % t, "K%d" % (t + 1), "PM" + s, "NR" + s, "SC" + s
        kw = (T[Kt][:, 0:M + 16], two(Kt) + [Kt + "s"])
        nrw = (T[NR][:], two(NR) + [NR + "s"])
        gather_a(NR, nxg, "s4_%d" % (t - 1))
        gather_a("KL", kw, "kl", 2)
        for j, (o, (src, wk, lk), c) in enumerate(pieces("LE", "kr", kw, 2)):
            tt(o, (src, wk + lk), buf("KL", 512 * j, 512 * j + 512, key=["KL#%d" % j]), A.is_ge, c, "g")
        diag(ps("P0"), "WH", "KL", 0, two("KL"), True, False)
        mm(ps("P0"), [("IH", b("nact" + s))], False, False)
        diag(ps("P0"), "WV", "LE", 0, two("LE"), False, True)
        f2, t2, uu, ng, ww = b("f2" + s), h("t2" + s), h("u" + s), b("ng" + s), h("w" + s)
        ts(b("f1" + s), ps("P0"), 9 * BIG, None, A.is_ge)
        ts(f2, ps("P0"), 16 * BIG + 255 * 129 - 0.5, None, A.is_ge)
        tt(t2, b("f1" + s), f("dlr"), A.mult)
        tt(uu, f2, f("vk"), A.mult)
        tt(ng, f2, nl, A.mult)
        own = [("IP", h("kr")), ("IP", t2), ("IP", uu)]
        mm(ps("P0", 64, 128), [("I1k", nl), ("I2k", f2)] + own + [("IN1k", ng)])
        cp(u("pm" + s), ps("P0", 64, 128))
        scatter("v", (T[PM][:], [PM]), "pm" + s, "IOA", cfg["sch"])
        tt(ww, ng, f("mv"), A.mult)
        own = own + [("IP", ww)]
        patch = t in cfg["patch"]
        if t < RO - 1 or patch:
            mm(ps("P7"), own)
            cp(u("src" + s), ps("P7"))
            gather_a(Kn, kw, "src" + s)
        if t == 0:
            cp(i32("si"), ps("P7"))
            ts(i32("sh"), i32("si"), 4, None, A.arith_shift_right)
            cp(b("sh"), i32("sh"))
            mm(ps("P7", 64, 128), [("I64", r) for W, r in own] + [("IN1k", b("sh")), ("IP", b("sh"))])
            cp(u("zt"), ps("P7", 64, 128))
            gather_a("ZG", (T.ZW[:], ["ZW", "ZW1"]), "zt")
            diag(ps("P7", 128, 192), "WH", "ZG", 0, two("ZG"), True, True)
            act(f("go0"), f2, -1.0, 1.0)
            tt(f("zd"), ps("P7", 128, 192), f("go0"), A.mult, 64)
            tt(f("Z2"), f("zd"), I["siz"], A.add)
        tk = b("tk" + s)
        diag(ps("P1"), "WN", PM, M, [PM], True, False)
        diag(ps("P1"), "WH", PM, 0, [PM], False, True)
        tt(f("ka" + s), ps("P1"), f("v128"), A.subtract, 64)
        ts(f("sk" + s), ps("P1"), 0.0, None, A.is_gt)
        ts(tk, ps("P1"), 0.0, None, A.not_equal)
        tt(h("kp" + s), f("ka" + s), f("sk" + s), A.mult)
        mm(ps("P1", 64, 128), own + [("IP", h("kp" + s))])
        cp(u("q" + s), ps("P1", 64, 128))
        nn = buf("NLS", t + 1, 256, 4, key=["NL%d" % (t + 1)])
        tt(nn, ng, tk, A.max)
        if t == RO - 1:
            tt(h("fa"), tk, f("mv"), A.mult)
            mm(ps("P7"), own + [("IP", h("fa"))])
            cp(u("fin"), ps("P7"))
            kf = "ZG" if patch else Kn
            gather_a(kf, kw, "fin")
            dma("s", T.yk[:], T[kf][:, 0:M], two(kf), ["yk"], 262144)
        else:
            act(f("ln" + s), nn, -1.0, 1.0)
            tt(f("zl" + s), f("Z2") if t else I["siz"], f("ln" + s), A.mult)
            tt(b("nact%d" % (t + 1)), f("zl" + s), f("T0") if t else f("T1"), A.is_ge)
            tt(f("nv" + s), nn, f("v16"), A.mult)

        def relink():
            gather_a("NQ", nrw, "q" + s)
            scatter("a", (T.NX[:], NXK), "sl" + s, "NQ", cfg["sch"])
        if not patch:
            relink()
        for k in range(1, 5):
            sk, sg = "s%d_%d" % (k, t), "SG%d" % (k % 2)
            bank = ps("P%d" % (2 + k % 2))
            sc = buf(SC, 5 - k, 320, 5, key=["%s_%d" % (SC, k)])
            top = BASE + (4 - k) * 4096.0 + 2048.0
            if k == 1 and patch:
                diag(ps("P2"), "WH", NR, 0, two(NR), True, True)
                act(f("na"), ps("P2"))
                gather_a("NP", nrw, "src" + s)
                diag(bank, "WH", "NP", 0, two("NP"), True, True)
                ts(u(sk), bank, -OFF, None, A.add)
                act(f("nb"), bank)
                act(sc, bank, -1.0, top + OFF)
                act(f("l0"), nl, -1.0, 1.0)
                tt(f("dn0"), f("na"), f("nb"), A.subtract)
                tt(f("dn"), f("dn0"), f("l0"), A.mult)
            elif k == 1:
                mm(bank, [("IH", tk)], True, False)
                diag(bank, "WQ", "NQ", 0, two("NQ"), False, True, slow=4)
                ts(u(sk), bank, -OFF, 2048.0, A.add, A.min)
                ts(sc, u(sk), -1.0, top, A.mult, A.add)
            elif patch:
                gather_a(sg, nxg, "s%d_%d" % (k - 1, t))
                if k == 4:
                    mm(bank, [("IH", tk)], True, False)
                diag(bank, "WH", sg, 0, two(sg), k < 4, True)
                tt(f("d1"), bank, f("nb"), A.is_equal, 64)
                tt(f("d2"), bank, f("na"), A.is_equal, 64)
                tt(f("d3"), f("d1"), f("d2"), A.subtract)
                tt(f("d4"), f("d3"), f("dn"), A.mult)
                tt(f("d5"), f("d4"), bank, A.add, 64)
                ts(u(sk), f("d5"), -OFF, 2048.0, A.add, A.min)
                ts(sc, u(sk), -1.0, top, A.mult, A.add)
            elif t in cfg["wch"]:
                gather_a(sg, nxg, "s%d_%d" % (k - 1, t), 2)
                for j in range(2):
                    hb = ps("P%d" % (2 + j), 0, 32)
                    diag(hb, "WH", sg, 512 * j, [sg + "#%d" % j], True, True, 32)
                    ts((tile("LU", sk, 32 * j, 32 * j + 32), ["u%s#%d" % (sk, j)]), hb, -OFF, None, A.add)
                ts(sc, u(sk), -1.0, top, A.mult, A.add)
            else:
                gather_a(sg, nxg, "s%d_%d" % (k - 1, t))
                diag(bank, "WH", sg, 0, two(sg), True, True)
                ts(u(sk), bank, -OFF, None, A.add)
                act(sc, bank, -1.0, top + OFF)
        r4 = buf("RS", t + 1, 256, 4, key=["RS%d" % (t + 1)])
        act(r4, sc, 1.0, -BASE)
        if patch:
            relink()
        if t < RO - 1:
            tt(f("sl" + s), f("nv" + s), r4, A.subtract)
            ts(u("sl%d" % (t + 1)), f("sl" + s), 2048.0, None, A.add)
        else:
            dma("s", T.OLO[:], T.NX[0::16, 0:IT], NXK, ["OLO"], 65536)
            dma("s", T.OHI[:], T.NX[1::16, 0:IT], NXK, ["OHI"], 65536)
            act(buf("OB", 0, 128, key=["OB0"]), buf("OHI"), n=128)
            act(buf("OB", 128, 256, key=["OB1"]), buf("OLO"), n=128)
            act(buf("OF", 0, 128, key=["OF0"]), buf("OB", 0, 128, key=["OB0"]), 128.0, -OFF, n=128)
            tt(buf("OF", 128, 256, key=["OF1"]), buf("OF", 0, 128, key=["OF0"]), buf("OB", 128, 256, key=["OB1"]), A.add, 256)
            dma("s", T.yn[:], T.OF[:, 128:256], ["OF1"], ["yn"], 65536)
            scan(buf("GS"), buf("NLS", key=["NLz", "NL1", "NL2", "NL3"]), buf("RS", key=["RS0", "RS1", "RS2", "RS3"]), A.mult, A.add, 256)
            act(buf("YC"), buf("GS", 3, 256, 4), -1.0, 2048.0)
            dma("s", T.yc[:], T.YC[:], ["YC"], ["yc"], 32768)
        nl = nn
        vb = "P%d" % (4 + t % 2)
        for k in range(1, 5):
            sk, cm = "s%d_%d" % (k, t), "CM%d" % (k - 1)
            way = []
            for j, (o, (src, wk, lk), c) in enumerate(pieces(cm, sk, xg, 2)):
                key = buf(Kn, 512 * j, 512 * j + 512, key=[Kn + "#%d" % j])
                if (t, k, j) in cfg["off"]:
                    xb = buf("XG%d" % (k % 2), 512 * j, 512 * j + 512, key=["XG%d#%d" % (k % 2, j)])
                    pb = ps("P7" if j else "P0", 0, 512)
                    plain(xb, (src, wk + lk), F.Copy, ("g", c))
                    mm(pb, [("IN", key), ("IP", xb)], n=512)
                    act(o, pb, 1.0, 0.5, 512, F.Sign)
                    way.append("WS")
                else:
                    tt(o, (src, wk + lk), key, A.is_lt, c, "g")
                    way.append("WV")
            for W, j0, j1 in ([(way[0], 0, 2)] if way[0] == way[1] else [(way[0], 0, 1), (way[1], 1, 2)]):
                out = buf(vb, 5 - k + 160 * j0, 160 * j1, 5)
                pre = []
                if W == "WS":
                    pre.append(("IH", b("quart", 32 * j0, 32 * j1)))
                if patch and k < 4:
                    pre.append(("INH", b("tk" + s, 32 * j0, 32 * j1)))
                if pre:
                    mm(out, pre, True, False)
                diag(out, W, cm, 512 * j0, two(cm)[j0:j1], not pre, True, 32 * (j1 - j0))
        scan(buf("M5"), ps(vb, 0, 320), buf(SC, key=[SC + "z"] + ["%s_%d" % (SC, k) for k in range(1, 5)]), A.max, A.min, 320)
        m = buf("M5", 4, 320, 5)
        ts(b("has" + s), m, BASE, None, A.is_gt)
        mm(ps("P6"), [("BO", b("has" + s))])
        mm(ps("P6", 64, 128), [("UP", b("has" + s))])
        ts(i32("lv" + s), m, -BASE, 0.0, A.add, A.max)
        ts(i32("lw" + s), i32("lv" + s), 4095, None, A.bitwise_and)
        cum = b("cum" + s)
        scan(cum, ps("P6"), b("c200"), A.add, A.min, 64)
        nv = 8 - cfg["acc"][t]
        for j in range(nv):
            ts(buf("F8", 64 * j, 64 * (j + 1), key=["F8%d" % j]), cum, -16.0 * j, col(2), A.add, A.is_le)
        if nv:
            scan(buf("CNT", 0, 64 * nv), buf("KEEP", 0, 64 * nv), buf("F8", 0, 64 * nv, key=["F8%d" % j for j in range(nv)]), A.mult, A.add, 32 * nv)
            ts((tile("LU", "ck" + s, 0, nv), ["cka"]), buf("CNT", 63, 64 * nv, 64), 63.0, None, A.min)
        for j in range(nv, 8):
            op("a", lambda q, j=j, s=s: q.activation(T.F8[:, 64 * j:64 * j + 63], tile("LB", "cum" + s, 0, 63), F.Sign, bias=tile("LF", "vh", j, j + 1),
                                                     scale=-1.0, accum_out=tile("LF", "cn" + s, j, j + 1)),
               cum[1] + ["fvh"], ["F8%d" % j, "cn%d" % j], ("e", 84))
        if nv < 8:
            ts((tile("LU", "ck" + s, nv, 8), ["ckb"]), (tile("LF", "cn" + s, nv, 8), ["cn%d" % j for j in range(nv, 8)]), 0.5, 31.5, A.mult, A.add)
        tt(b("pl" + s), cum, ps("P6", 64, 128), A.subtract, 64)
        ck = tile("LU", "ck" + s, 0, 8)
        tt(buf("EQ"), (tile("LB", "pl" + s).indirect(ck), ["cka", "ckb", "bpl" + s]), buf("KIO"), A.is_equal, 128, "g")
        tt(buf("SEL"), (tile("LI", "lw" + s).indirect(ck), ["cka", "ckb", "ilw" + s]), buf("EQ"), A.mult, 128, "g")
        e1 = ps("P6", 128, 136)
        diag(e1, "W1", "SEL", 0, ["SEL"], True, True, 8)
        ts(u8("eo" + s), e1, -1.0, 2048.0, A.mult, A.add)
        cp(buf("SND" + s), (xg[0].indirect(u8("eo" + s)[0]), xg[1] + ["ueo" + s]), 128, "g")
        op("g", lambda q, t=t: send(q, t), ["SND" + s], ["RCV" + s], ("r", t))
        ts(f("e0" + s, 0, 8), e1, 0.0, None, A.is_equal)
        tt(f("e1" + s, 0, 8), f("e0" + s, 0, 8), f("v16", 0, 8), A.mult, 64)
        tt(f("e2" + s, 0, 8), f("e1" + s, 0, 8), e1, A.subtract, 64)
        ts(u8("es" + s), f("e2" + s, 0, 8), 2048.0, None, A.add)
        d0, d1, d2 = [buf("DD", 128 * j, 128 * (j + 1), key=["D%d" % j]) for j in range(3)]
        act(d0, buf("SND" + s), 1.0, -255.0, 128)
        ts(d1, buf("RCV" + s), 255.0, None, A.is_ge)
        tt(d2, d1, d0, A.mult, 256)
        tt((T.X[:].indirect(u8("es" + s)[0]), ["X", "Xs"]), buf("RCV" + s), (d2[0], d2[1] + ["ues" + s]), A.add, 128, "s")
    dma("s", T.yx[:], T.X[:, 0:IT], ["X"], ["yx"], 524288)
    return ops


def depend(ops):
    last, readers, deps = {}, {}, []
    for j, o in enumerate(ops):
        d = {}

        def add(i):
            d[i] = not (ops[i]["eng"] == "p" and o["eng"] == "p")
        for k in o["r"]:
            if k in last:
                add(last[k])
            if k[0] == "P" and k[1:].isdigit():
                for i in readers.get(k, []):
                    if ops[i]["eng"] != o["eng"]:
                        add(i)
        for k in o["w"]:
            if k in last:
                add(last[k])
            for i in readers.get(k, []):
                if i != j:
                    add(i)
        for k in o["r"]:
            readers.setdefault(k, []).append(j)
        for k in o["w"]:
            last[k] = j
            readers[k] = []
        deps.append(d)
    return deps


def rank_program(g, core, T, topo):
    rank = T.rank_of(core)
    if rank is None:
        return
    dst = T.cores[(rank + 1) % len(T.cores)]
    rid, pid = topo.addr(dst, core)
    mask = topo.mask(core, dst)
    prev = T.cores[(rank - 1) % len(T.cores)]
    nin = len(topo.engines(prev, core))
    nout = len(topo.engines(core, dst))

    def send(q, t):
        return q.remote_dma(T["RCV%d" % t][:], T["SND%d" % t][:], T.sem["arr%d" % t], T.sem.sent, pid, rid, mask)

    ops = build(T, send, CFG)
    deps = depend(ops)
    queue = {"v": g.vector, "a": g.scalar, "p": g.tensor, "g": g, "s": g.sync}
    awaited = set(i for d in deps for i, w in d.items() if w)
    mark, count, seen, nd = {}, {}, {e: {} for e in queue}, [0]
    for j in ORDER:
        o = ops[j]
        e, q = o["eng"], queue[o["eng"]]
        need = {}
        for i, w in deps[j].items():
            if w:
                sem, val = mark[i]
                need[sem] = max(need.get(sem, 0), val)
        for sem, val in need.items():
            if seen[e].get(sem, 0) < val:
                q.wait_ge(T.sem[sem], val)
                seen[e][sem] = val
        ins = o["fn"](q)
        kind = o["c"][0]
        if kind == "r":
            sem = "arr%d" % o["c"][1]
            count[sem] = nin
            count["sent"] = count.get("sent", 0) + nout
        elif kind == "d":
            sem = "d%d" % nd[0]
            nd[0] += 1
            count[sem] = 16
            ins.then_inc(T.sem[sem], 16)
        elif j in awaited:
            sem = "e" + e
            count[sem] = count.get(sem, 0) + 1
            ins.then_inc(T.sem[sem], 1)
        else:
            continue
        mark[j] = (sem, count[sem])
    for sem, val in count.items():
        if max(seen[e].get(sem, 0) for e in queue) < val:
            g.wait_ge(T.sem[sem], val)
